import numpy as np
import ml_dtypes


def mxq(x, axis, fmt="e4m3"):
    dtype, down = {"e4m3": (ml_dtypes.float8_e4m3fn, 7), "e5m2": (ml_dtypes.float8_e5m2, 14)}[fmt]
    v = np.moveaxis(np.asarray(x, np.float32).astype(ml_dtypes.bfloat16).astype(np.float64), axis, -1)
    blocks = v.reshape(v.shape[:-1] + (-1, 32))
    amax = np.abs(blocks).max(-1, keepdims=True)
    byte = np.maximum(np.where(amax > 0, np.frexp(amax)[1] - 1 + 127, 0) - down, 1)
    scale = np.exp2(byte - 127.0)
    codes = (blocks / scale).astype(np.float32).astype(dtype).astype(np.float64)
    return np.moveaxis((codes * scale).reshape(v.shape), -1, axis)


WIDE = False


def mx_kscale(k):
    if not WIDE:
        return np.ones(k)
    levels = np.array([10, -10, 5, -5, 0])
    if k % 512:
        return np.exp2(np.random.permutation(np.resize(levels, k // 32))).repeat(32)
    a = np.empty((k // 512, 16))
    for p in range(k // 512):
        a[p, :8] = np.random.permutation(np.resize(levels, 8))
        for g in range(8):
            far = levels[np.abs(levels - a[p, g]) >= 10]
            a[p, g + 8] = far[np.random.randint(len(far))]
    return np.exp2(a.ravel()).repeat(32)


def f64(x):
    return np.asarray(x).astype(np.float64)


def striped(idx):
    return np.tile(idx.reshape(-1, 16).T, (8, 1)).astype(np.uint16)


def unstriped(offs):
    return offs[:16].T.reshape(-1).astype(np.int64)


E2M1 = np.array([0.0, 0.5, 1.0, 1.5, 2.0, 3.0, 4.0, 6.0, -0.0, -0.5, -1.0, -1.5, -2.0, -3.0, -4.0, -6.0])


def pack_weight(w, fmt):
    k, n = w.shape
    w = f64(np.asarray(w, np.float32).astype(ml_dtypes.bfloat16)).reshape(k // 32, 32, n)
    amax = np.abs(w).max(1)
    if fmt == "e4m3":
        byte = np.frexp(amax)[1] - 1 + 127 - 7
    else:
        mant, ex = np.frexp(amax / 6.0)
        byte = np.where(mant > 0.5, ex, ex - 1) + 127
    byte = np.clip(np.where(amax > 0, byte, 1), 1, 254)
    scaled = (w * np.exp2(127.0 - byte)[:, None, :]).reshape(k, n).astype(np.float32)
    by_word = np.ascontiguousarray(scaled.reshape(k // 512, 128, 4, n).transpose(0, 1, 3, 2))
    if fmt == "e4m3":
        words = by_word.astype(ml_dtypes.float8_e4m3fn).view(np.uint8)
    else:
        c = by_word.astype(ml_dtypes.float4_e2m1fn).view(np.uint8) & 0xF
        words = (c[..., 0::2] | (c[..., 1::2] << 4)).reshape(k // 512, 128, 2 * n)
    return np.ascontiguousarray(words), np.ascontiguousarray(byte.astype(np.uint8).reshape(k // 512, 16, n))


def unpack_weight(words, scales, fmt):
    g, _, n = scales.shape
    words = np.ascontiguousarray(words).reshape(g, 128, n, -1)
    if fmt == "e4m3":
        vals = words.view(ml_dtypes.float8_e4m3fn).astype(np.float64)
    else:
        nib = np.empty((g, 128, n, 4), np.uint8)
        nib[..., 0::2] = words & 0xF
        nib[..., 1::2] = words >> 4
        vals = E2M1[nib]
    vals = vals * np.repeat(np.exp2(scales.astype(np.float64) - 127.0), 8, axis=1)[..., None]
    return vals.transpose(0, 1, 3, 2).reshape(g * 512, n)


def gelu(v):
    return 0.5 * v * (1.0 + np.tanh(np.sqrt(2.0 / np.pi) * (v + 0.044715 * v**3)))


def striped8(idx):
    return np.concatenate([v.reshape(-1, 16).T for v in idx]).astype(np.uint16)


def unstriped8(offs):
    return np.stack([offs[16 * g:16 * g + 16].T.reshape(-1) for g in range(8)]).astype(np.int64)


def heads(xT, wgt, idx8):
    k = np.arange(xT.shape[0])
    return wgt[k // 4 % 128] * xT[k[:, None], idx8[k % 512 // 64]]


K, T, S, R, N = 1024, 2048, 1024, 512, 768

def setup_inputs():
    n = np.random.standard_normal
    s = mx_kscale(K)[:, None]
    u = mx_kscale(S)[:, None]
    wv_words, wv_scales = pack_weight(n((K, N)) / np.sqrt(K) / s, "e2m1")
    return {
        "xT": (n((K, T)) * s).astype(np.float32),
        "wgt": np.repeat(np.random.uniform(0.5, 2.0, (8, S)), 16, axis=0).astype(np.float32),
        "offs": striped8(np.stack([np.random.permutation(T)[:S] for _ in range(8)])),
        "wk": (0.5 * n((K, R)) / np.sqrt(K) / s).astype(np.float32),
        "wv_words": wv_words,
        "wv_scales": wv_scales,
        "keep": (np.random.uniform(0.5, 1.5, S) / S ** 0.25 * u[:, 0]).astype(np.float32),
        "beta": (np.random.uniform(0.5, 1.5, S) / S ** 0.25 / u[:, 0]).astype(np.float32),
        "lam": np.random.uniform(0.5, 0.95, N).astype(np.float32),
        "old": n((N, R)).astype(np.float32),
    }

def reference(xT, wgt, offs, wk, wv_words, wv_scales, keep, beta, lam, old):
    xg = heads(f64(xT), f64(wgt), unstriped8(offs))
    xq = mxq(xg, 0, "e4m3")
    key = np.exp(xq.T @ mxq(f64(wk), 0, "e4m3")) * f64(keep)[:, None]
    wv = unpack_weight(wv_words, wv_scales, "e2m1")
    val = (xq.T @ wv) * f64(beta)[:, None]
    write = mxq(val, 0, "e4m3").T @ mxq(key, 0, "e4m3")
    return f64(lam)[:, None] * f64(old) + write

@@ -1,0 +1,281 @@
+import math
+from contextlib import ExitStack
+
+import concourse.mybir as mybir
+from concourse.masks import make_identity
+
+K, T, S, R, N = 1024, 2048, 1024, 512, 768
+FLOPS = 2 * K * S * R + 2 * K * S * N + 2 * S * N * R
+
+F32 = mybir.dt.float32
+BF16 = mybir.dt.bfloat16
+I32 = mybir.dt.int32
+U32 = mybir.dt.uint32
+U16 = mybir.dt.uint16
+U8 = mybir.dt.uint8
+E4M3 = mybir.dt.float8_e4m3fn_x4
+E2M1 = mybir.dt.float4_e2m1fn_x4
+ALU = mybir.AluOpType
+ACT = mybir.ActivationFunctionType
+
+P = 128
+PACK = 4
+PASS = P * PACK
+KP = K // PASS
+SP = S // PASS
+NT = N // P
+H = R // 2
+
+ORDER = """
+g000:V g001:V g010:V g011:V g021:V g020:V g030:V g031:V c:V f001:S g101:V f000:S g100:V f010:S g111:V f011:S
+g110:V p1:S g120:V p0:S qx00:V g130:V g131:V f101:S f100:V qx101:V qx100:V w10:S g121:V vm03:P w00:S qw10:V
+qx01:V vm01:P w01:V f110:S vm02:P qw00:V vs03:S qw01:V z001:P qx110:V f111:S vd02:V z100:P vd01:V z000:P
+e001:S qx111:V vm05:P w11:V e100:S z101:P e000:S qv01:V qv02:V qw11:V vm10:P vd03:V vs05:S k00:V z010:P e101:S
+z111:P qv03:V vd10:V e010:S z011:P qk00:V qv10:V e111:S z110:P k10:V vm13:P e011:S vd05:V qk10:V vm15:P e110:S
+vd13:V vm04:P k01:S vd15:V vm00:P qv13:V vd04:V fm30:P k11:S vm12:P qk01:V qv04:V qv5:V vm11:P st30:V vs00:S
+vd12:V fm50:P vm14:P qk11:V vs11:S vd00:V fm51:P st50:V vs14:S fm31:P qv00:V st51:V fm00:P st31:V vd11:S
+fm01:P qv12:V st00:V vd14:S fm20:P st01:V fm21:P qv11:V st20:V fm10:P qv14:V st21:V fm11:P st10:V fm41:P
+fm40:P st11:V st41:V st40:V
+""".split()
+
+
+def tile_list_fast_weight_write_kernel(tc, xT, wgt, offs, wk, wv_words, wv_scales, keep, beta, lam, old, out):
+    nc = tc.nc
+    with ExitStack() as ctx:
+        held = ctx.enter_context(tc.tile_pool(name="held", bufs=1))
+        psum = ctx.enter_context(tc.psum_pool(name="psum", bufs=8))
+
+        def sb(name, shape, dtype):
+            return held.tile(shape, dtype, name=name, align_bytes=64)
+
+        def new_bank():
+            return psum.tile([P, 512], F32, name="bank")
+
+        offsets = held.tile([P, S // 16], U16, name="offsets")
+        planes = [[sb(f"plane{a}{i}", [P, T], F32) for i in range(PACK)] for a in range(KP)]
+        weights = [sb(f"weights{b}", [P, PASS], F32) for b in range(SP)]
+        wk_raw = [[sb(f"wk_raw{a}{h}", [P, PACK, H], F32) for h in range(2)] for a in range(KP)]
+        wv_codes = sb("wv_codes", [P, KP, 2 * N], U8)
+        wv_plane = sb("wv_plane", [P, KP, N], U8)
+        rows = sb("rows", [P, SP * P], F32)
+        identity = sb("identity", [P, P], F32)
+        state = [sb(f"state{c}", [P, R], F32) for c in range(NT)]
+
+        nc.gpsimd.memset(rows[:], 0.0)
+        nc.gpsimd.memset(wv_plane[:].rearrange("p a n -> p (a n)").bitcast(I32), 0)
+        make_identity(nc, identity[:])
+
+        x_planes = xT.rearrange("(a p i) t -> a i p t", a=KP, i=PACK)
+        wk_rows = wk.rearrange("(a p i) r -> a p i r", a=KP, i=PACK)
+
+        def load_plane(a, i):
+            nc.sync.dma_start(planes[a][i][:], x_planes[a, i])
+
+        def load_slot_rows(first, vec):
+            nc.sync.dma_start(
+                rows[first : first + PACK, :].rearrange("t (m e) -> t m e", e=4),
+                vec.rearrange("(m t e) -> t m e", t=PACK, e=4),
+            )
+
+        def load_wv_scales(q):
+            nc.sync.dma_start(
+                wv_plane[32 * q : 32 * q + 4].bitcast(I32),
+                wv_scales[:, 4 * q : 4 * q + 4, :].rearrange("a r n -> r a n").bitcast(I32),
+            )
+
+        nc.sync.dma_start(offsets[:], offs)
+        load_plane(0, 0)
+        nc.sync.dma_start(weights[0][:], wgt[:, 0:PASS])
+        nc.sync.dma_start(weights[1][:], wgt[:, PASS:S])
+        load_plane(0, 1)
+        load_slot_rows(0, keep)
+        load_plane(0, 2)
+        load_slot_rows(PACK, beta)
+        load_plane(0, 3)
+        nc.sync.dma_start(rows[8:12, 0:P], lam[0 : 4 * P].rearrange("(c p) -> c p", p=P))
+        load_plane(1, 0)
+        nc.sync.dma_start(rows[12:14, 0:P], lam[4 * P : N].rearrange("(c p) -> c p", p=P))
+        load_wv_scales(0)
+        load_plane(1, 1)
+        load_wv_scales(1)
+        load_wv_scales(2)
+        load_plane(1, 2)
+        load_wv_scales(3)
+        load_plane(1, 3)
+        nc.sync.dma_start(wv_codes[:].bitcast(I32), wv_words.rearrange("a p n -> p a n").bitcast(I32))
+        for h in range(2):
+            for a in (1, 0):
+                nc.sync.dma_start(wk_raw[a][h][:], wk_rows[a][:, :, h * H : (h + 1) * H])
+        for c in range(NT):
+            nc.sync.dma_start(state[c][:], old[c * P : (c + 1) * P, :])
+
+        factors = sb("factors", [P, SP, 16], F32)
+        ln_keep = sb("ln_keep", [P, SP, PACK], F32)
+        signed_beta = sb("signed_beta", [P, SP, PACK], F32)
+
+        def make_factors():
+            turned = new_bank()
+            for b in range(SP):
+                nc.tensor.transpose(turned[:, b * P : (b + 1) * P], rows[:, b * P : (b + 1) * P], identity[:])
+            nc.scalar.copy(factors[:], turned[:, 0 : SP * P].rearrange("p (b c) -> p b c", b=SP)[:, :, 0:16])
+            keep_f = factors[:, :, 0:PACK]
+            beta_f = factors[:, :, PACK : 2 * PACK]
+            expo = sb("expo", [P, SP, PACK], I32)
+            mant = sb("mant", [P, SP, PACK], I32)
+            ln_expo = sb("ln_expo", [P, SP, PACK], F32)
+            ln_mant = sb("ln_mant", [P, SP, PACK], F32)
+            twice_pos = sb("twice_pos", [P, SP, PACK], F32)
+            nc.vector.tensor_scalar(mant[:], keep_f.bitcast(I32), 0x7FFFFF, 0x3F800000, ALU.bitwise_and, ALU.bitwise_or)
+            nc.vector.tensor_scalar(expo[:], keep_f.bitcast(I32), 23, 0xFF, ALU.logical_shift_right, ALU.bitwise_and)
+            nc.vector.tensor_scalar(twice_pos[:], keep_f, 0.0, 2.0, ALU.is_ge, ALU.mult)
+            nc.scalar.activation(ln_mant[:], mant[:].bitcast(F32), ACT.Ln)
+            nc.vector.tensor_scalar(ln_expo[:], expo[:], -127.0, math.log(2.0), ALU.add, ALU.mult)
+            nc.vector.scalar_tensor_tensor(signed_beta[:], twice_pos[:], -1.0, beta_f, ALU.add, ALU.mult)
+            nc.vector.tensor_tensor(ln_keep[:], ln_mant[:], ln_expo[:], ALU.add)
+
+        def mx_pair(name, width):
+            return sb(name + "_codes", [P, width], U32), sb(name + "_scales", [P, width], U8)
+
+        picked = [[sb(f"picked{a}{b}", [P, PACK, PASS], F32) for b in range(SP)] for a in range(KP)]
+        xg = [[sb(f"xg{a}{b}", [P, PACK * PASS], BF16) for b in range(SP)] for a in range(KP)]
+        xq = [[mx_pair(f"xq{a}{b}", PASS) for b in range(SP)] for a in range(KP)]
+        wkg = [[sb(f"wkg{a}{h}", [P, PACK * H], BF16) for h in range(2)] for a in range(KP)]
+        wkq = [[mx_pair(f"wkq{a}{h}", H) for h in range(2)] for a in range(KP)]
+        key_rows = [[sb(f"key_rows{b}{h}", [P, PACK, H], BF16) for h in range(2)] for b in range(SP)]
+        keyg = [[sb(f"keyg{b}{h}", [P, PACK * H], BF16) for h in range(2)] for b in range(SP)]
+        keyq = [mx_pair(f"keyq{b}", R) for b in range(SP)]
+        valg = [sb(f"valg{c}", [P, SP * PASS], BF16) for c in range(NT)]
+        valq = [mx_pair(f"valq{c}", SP * P) for c in range(NT)]
+        val_rows = {}
+        banks = {}
+        copy_on = {"S": nc.scalar.copy, "V": nc.vector.tensor_copy}
+
+        def quantise(pair, first, width, grouped):
+            cols = slice(first, first + width)
+            nc.vector.quantize_mx(pair[0][:, cols].bitcast(E4M3), pair[1][:, cols], grouped)
+
+        def interleave(engine, dst, src):
+            copy_on[engine](
+                dst.rearrange("p (c e t) -> p c t e", t=PACK, e=4),
+                src.rearrange("p t (c e) -> p c t e", e=4),
+            )
+
+        def group_x(engine, a, b, tiles, lanes):
+            dst = xg[a][b][:].rearrange("p (t m e i) -> p m t e i", t=PACK, e=4, i=PACK)
+            src = picked[a][b][:].rearrange("p i (m t e) -> p m t e i", t=PACK, e=4)
+            copy_on[engine](dst[:, :, tiles, :, lanes], src[:, :, tiles, :, lanes])
+
+        def group_x_all(engine, a, b, tiles):
+            dst = xg[a][b][:].rearrange("p (t m e i) -> p m t i e", t=PACK, e=4, i=PACK)
+            src = picked[a][b][:].rearrange("p i (m t e) -> p m t i e", t=PACK, e=4)
+            copy_on[engine](dst[:, :, tiles], src[:, :, tiles])
+
+        def mx(dst, left, lcols, right_codes, right_scales, start, stop):
+            nc.tensor.matmul_mx(
+                dst,
+                lhsT=left[0][:, lcols].bitcast(E4M3),
+                lhsT_scale=left[1][:, lcols],
+                rhs=right_codes,
+                rhs_scale=right_scales,
+                start=start,
+                stop=stop,
+            )
+
+        for step in ORDER:
+            word, engine = step.split(":")
+            kind = "".join(ch for ch in word if ch not in "0123456789")
+            n = [int(ch) for ch in word if ch in "0123456789"]
+            if kind == "c":
+                make_factors()
+            elif kind == "g":
+                a, i, b = n
+                cols = slice(b * PASS // 16, (b + 1) * PASS // 16)
+                nc.vector.tensor_tensor(picked[a][b][:, i, :], planes[a][i][:].indirect(offsets[:, cols]), weights[b][:], ALU.mult)
+            elif kind == "p":
+                group_x(engine, 1, n[0], slice(0, 4), slice(0, 2))
+            elif kind == "f":
+                a, b, h = n
+                if a == 0 or not True:
+                    group_x_all(engine, a, b, slice(2 * h, 2 * h + 2))
+                else:
+                    group_x(engine, a, b, slice(2 * h, 2 * h + 2), slice(2, 4))
+            elif kind == "qx" and len(n) == 2:
+                quantise(xq[n[0]][n[1]], 0, PASS, xg[n[0]][n[1]][:])
+            elif kind == "qx":
+                a, b, h = n
+                quantise(xq[a][b], h * 256, 256, xg[a][b][:, h * 1024 : (h + 1) * 1024])
+            elif kind == "w":
+                a, h = n
+                interleave(engine, wkg[a][h][:], wk_raw[a][h][:])
+            elif kind == "qw":
+                a, h = n
+                quantise(wkq[a][h], 0, H, wkg[a][h][:])
+            elif kind == "z":
+                b, h, u = n
+                bank = new_bank()
+                banks["z", b, h, u] = bank
+                for d in range(2):
+                    t = 2 * u + d
+                    for a in range(KP):
+                        mx(bank[:, d * H : (d + 1) * H], xq[a][b], slice(t * P, (t + 1) * P),
+                           wkq[a][h][0][:].bitcast(E4M3), wkq[a][h][1][:], a == 0, a == KP - 1)
+            elif kind == "e":
+                b, h, u = n
+                bank = banks["z", b, h, u]
+                for d in range(2):
+                    t = 2 * u + d
+                    nc.scalar.activation(key_rows[b][h][:, t, :], bank[:, d * H : (d + 1) * H], ACT.Exp, bias=ln_keep[:, b, t : t + 1])
+            elif kind == "k":
+                b, h = n
+                interleave(engine, keyg[b][h][:], key_rows[b][h][:])
+            elif kind == "qk":
+                b, h = n
+                quantise(keyq[b], h * H, H, keyg[b][h][:])
+            elif kind == "vm":
+                b, c = n
+                bank = new_bank()
+                banks["v", b, c] = bank
+                for t in range(PACK):
+                    for a in range(KP):
+                        mx(bank[:, t * P : (t + 1) * P], xq[a][b], slice(t * P, (t + 1) * P),
+                           wv_codes[:, a, 2 * c * P : 2 * (c + 1) * P].bitcast(E2M1), wv_plane[:, a, c * P : (c + 1) * P],
+                           a == 0, a == KP - 1)
+            elif kind == "vs":
+                b, c = n
+                val_rows[b, c] = sb(f"val_rows{b}{c}", [P, PACK, P], BF16)
+                for t in range(PACK):
+                    nc.scalar.activation(val_rows[b, c][:, t, :], banks["v", b, c][:, t * P : (t + 1) * P], ACT.Copy,
+                                         scale=signed_beta[:, b, t : t + 1])
+            elif kind == "vd":
+                b, c = n
+                dst = valg[c][:, b * PASS : (b + 1) * PASS]
+                if (b, c) in val_rows:
+                    interleave(engine, dst, val_rows[b, c][:])
+                else:
+                    nc.vector.tensor_tensor(
+                        dst.rearrange("p (n t) -> p n t", t=PACK),
+                        banks["v", b, c][:].rearrange("p (t n) -> p n t", t=PACK),
+                        signed_beta[:, b, :].unsqueeze(1).broadcast_to([P, P, PACK]),
+                        ALU.mult,
+                    )
+            elif kind == "qv" and len(n) == 1:
+                quantise(valq[n[0]], 0, SP * P, valg[n[0]][:])
+            elif kind == "qv":
+                b, c = n
+                quantise(valq[c], b * P, P, valg[c][:, b * PASS : (b + 1) * PASS])
+            elif kind == "fm":
+                c = n[0]
+                cols = slice(0, R) if len(n) == 1 else slice(n[1] * H, (n[1] + 1) * H)
+                bank = new_bank()
+                banks["o", word] = bank
+                for b in range(SP):
+                    mx(bank[:, cols], valq[c], slice(b * P, (b + 1) * P),
+                       keyq[b][0][:, cols].bitcast(E4M3), keyq[b][1][:, cols], b == 0, b == SP - 1)
+            else:
+                c = n[0]
+                cols = slice(0, R) if len(n) == 1 else slice(n[1] * H, (n[1] + 1) * H)
+                nc.vector.scalar_tensor_tensor(
+                    state[c][:, cols], state[c][:, cols], factors[:, 0, 8 + c : 9 + c],
+                    banks["o", "fm" + word[2:]][:, cols], ALU.mult, ALU.add,
+                )
+                nc.sync.dma_start(out[c * P : (c + 1) * P, cols], state[c][:, cols])

@@ -2,7 +2,6 @@ import math
 from contextlib import ExitStack
 
 import concourse.mybir as mybir
-from concourse.masks import make_identity
 
 K, T, S, R, N = 1024, 2048, 1024, 512, 768
 FLOPS = 2 * K * S * R + 2 * K * S * N + 2 * S * N * R
@@ -27,15 +26,14 @@ NT = N // P
 H = R // 2
 
 ORDER = """
-g000:V g001:V g010:V g011:V g021:V g020:V g030:V g031:V c:V f001:S g101:V f000:S g100:V f010:S g111:V f011:S
-g110:V p1:S g120:V p0:S qx00:V g130:V g131:V f101:S f100:V qx101:V qx100:V w10:S g121:V vm03:P w00:S qw10:V
-qx01:V vm01:P w01:V f110:S vm02:P qw00:V vs03:S qw01:V z001:P qx110:V f111:S vd02:V z100:P vd01:V z000:P
-e001:S qx111:V vm05:P w11:V e100:S z101:P e000:S qv01:V qv02:V qw11:V vm10:P vd03:V vs05:S k00:V z010:P e101:S
-z111:P qv03:V vd10:V e010:S z011:P qk00:V qv10:V e111:S z110:P k10:V vm13:P e011:S vd05:V qk10:V vm15:P e110:S
-vd13:V vm04:P k01:S vd15:V vm00:P qv13:V vd04:V fm30:P k11:S vm12:P qk01:V qv04:V qv5:V vm11:P st30:V vs00:S
-vd12:V fm50:P vm14:P qk11:V vs11:S vd00:V fm51:P st50:V vs14:S fm31:P qv00:V st51:V fm00:P st31:V vd11:S
-fm01:P qv12:V st00:V vd14:S fm20:P st01:V fm21:P qv11:V st20:V fm10:P qv14:V st21:V fm11:P st10:V fm41:P
-fm40:P st11:V st41:V st40:V
+g000:V g001:V g010:V g011:V c:V g021:V g020:V g030:V g031:V r0:S g100:V g110:V r1:S g111:V g120:V qx01:V
+g130:V g131:V f100:S qx00:V f101:S g101:V w00:S qx10:V g121:V w10:S vm04:P w11:V w01:S vm02:P qw0:V vd04:V
+f110:S vm03:P vd02:V vm05:P qw1:V f111:S z000:P vd05:V z001:P qv04:V z011:P e000:S vd03:V z010:P qv05:V e001:S
+qx11:V vm00:P e011:S qu01:V vm01:P k00:V e010:S vm12:P vd00:V z111:P vd01:V k01:S vm11:P vd12:V z110:P vd11:V
+e111:S vm10:P qu00:V vm14:P e110:S qk01:V vd10:V vm15:P qk00:V k11:S z101:P qu10:V vd15:V z100:P e101:S vm13:P
+vd14:V qk11:V e100:S vd13:V fm11:P fm01:P qu12:V k10:S st11:V fm51:P st01:V fm41:P qu11:V st51:V fm21:P qk10:V
+fm31:P st41:V fm30:P st21:V fm50:P st31:V fm20:P st30:V fm40:P st50:V fm00:P fm10:P st40:V st00:V st10:V
+st20:V
 """.split()
 
 
@@ -57,13 +55,12 @@ def tile_list_fast_weight_write_kernel(tc, xT, wgt, offs, wk, wv_words, wv_scale
         wk_raw = [[sb(f"wk_raw{a}{h}", [P, PACK, H], F32) for h in range(2)] for a in range(KP)]
         wv_codes = sb("wv_codes", [P, KP, 2 * N], U8)
         wv_plane = sb("wv_plane", [P, KP, N], U8)
-        rows = sb("rows", [P, SP * P], F32)
-        identity = sb("identity", [P, P], F32)
+        keep_f = sb("keep_f", [P, SP, PACK], F32)
+        beta_f = sb("beta_f", [P, SP, PACK], F32)
+        lam_f = sb("lam_f", [P, NT], F32)
         state = [sb(f"state{c}", [P, R], F32) for c in range(NT)]
 
-        nc.gpsimd.memset(rows[:], 0.0)
         nc.gpsimd.memset(wv_plane[:].rearrange("p a n -> p (a n)").bitcast(I32), 0)
-        make_identity(nc, identity[:])
 
         x_planes = xT.rearrange("(a p i) t -> a i p t", a=KP, i=PACK)
         wk_rows = wk.rearrange("(a p i) r -> a p i r", a=KP, i=PACK)
@@ -71,66 +68,52 @@ def tile_list_fast_weight_write_kernel(tc, xT, wgt, offs, wk, wv_words, wv_scale
         def load_plane(a, i):
             nc.sync.dma_start(planes[a][i][:], x_planes[a, i])
 
-        def load_slot_rows(first, vec):
-            nc.sync.dma_start(
-                rows[first : first + PACK, :].rearrange("t (m e) -> t m e", e=4),
-                vec.rearrange("(m t e) -> t m e", t=PACK, e=4),
-            )
+        def load_wk(h):
+            for a in range(KP):
+                nc.sync.dma_start(wk_raw[a][h][:], wk_rows[a][:, :, h * H : (h + 1) * H])
 
-        def load_wv_scales(q):
-            nc.sync.dma_start(
+        nc.gpsimd.dma_start(keep_f[:], keep.rearrange("(b p t) -> p b t", b=SP, t=PACK))
+        nc.gpsimd.dma_start(beta_f[:], beta.rearrange("(b p t) -> p b t", b=SP, t=PACK))
+        for q in range(4):
+            nc.gpsimd.dma_start(
                 wv_plane[32 * q : 32 * q + 4].bitcast(I32),
                 wv_scales[:, 4 * q : 4 * q + 4, :].rearrange("a r n -> r a n").bitcast(I32),
             )
 
         nc.sync.dma_start(offsets[:], offs)
-        load_plane(0, 0)
-        nc.sync.dma_start(weights[0][:], wgt[:, 0:PASS])
-        nc.sync.dma_start(weights[1][:], wgt[:, PASS:S])
-        load_plane(0, 1)
-        load_slot_rows(0, keep)
-        load_plane(0, 2)
-        load_slot_rows(PACK, beta)
-        load_plane(0, 3)
-        nc.sync.dma_start(rows[8:12, 0:P], lam[0 : 4 * P].rearrange("(c p) -> c p", p=P))
-        load_plane(1, 0)
-        nc.sync.dma_start(rows[12:14, 0:P], lam[4 * P : N].rearrange("(c p) -> c p", p=P))
-        load_wv_scales(0)
-        load_plane(1, 1)
-        load_wv_scales(1)
-        load_wv_scales(2)
-        load_plane(1, 2)
-        load_wv_scales(3)
-        load_plane(1, 3)
-        nc.sync.dma_start(wv_codes[:].bitcast(I32), wv_words.rearrange("a p n -> p a n").bitcast(I32))
-        for h in range(2):
-            for a in (1, 0):
-                nc.sync.dma_start(wk_raw[a][h][:], wk_rows[a][:, :, h * H : (h + 1) * H])
+        for item in "x00 wA wB x01 x02 x03 x10 x11 x12 x13 wv wk0 wk1".split():
+            if item[0] == "x":
+                load_plane(int(item[1]), int(item[2]))
+            elif item == "wA":
+                nc.sync.dma_start(weights[0][:], wgt[:, 0:PASS])
+            elif item == "wB":
+                nc.sync.dma_start(weights[1][:], wgt[:, PASS:S])
+            elif item == "wv":
+                nc.sync.dma_start(wv_codes[:].bitcast(I32), wv_words.rearrange("a p n -> p a n").bitcast(I32))
+            else:
+                load_wk(int(item[2]))
+        with nc.allow_non_contiguous_dma(reason="one decay factor to a partition"):
+            nc.sync.dma_start(lam_f[:], lam.rearrange("(c p) -> p c", p=P))
         for c in range(NT):
             nc.sync.dma_start(state[c][:], old[c * P : (c + 1) * P, :])
 
-        factors = sb("factors", [P, SP, 16], F32)
         ln_keep = sb("ln_keep", [P, SP, PACK], F32)
         signed_beta = sb("signed_beta", [P, SP, PACK], F32)
 
         def make_factors():
-            turned = new_bank()
-            for b in range(SP):
-                nc.tensor.transpose(turned[:, b * P : (b + 1) * P], rows[:, b * P : (b + 1) * P], identity[:])
-            nc.scalar.copy(factors[:], turned[:, 0 : SP * P].rearrange("p (b c) -> p b c", b=SP)[:, :, 0:16])
-            keep_f = factors[:, :, 0:PACK]
-            beta_f = factors[:, :, PACK : 2 * PACK]
             expo = sb("expo", [P, SP, PACK], I32)
             mant = sb("mant", [P, SP, PACK], I32)
             ln_expo = sb("ln_expo", [P, SP, PACK], F32)
             ln_mant = sb("ln_mant", [P, SP, PACK], F32)
             twice_pos = sb("twice_pos", [P, SP, PACK], F32)
-            nc.vector.tensor_scalar(mant[:], keep_f.bitcast(I32), 0x7FFFFF, 0x3F800000, ALU.bitwise_and, ALU.bitwise_or)
-            nc.vector.tensor_scalar(expo[:], keep_f.bitcast(I32), 23, 0xFF, ALU.logical_shift_right, ALU.bitwise_and)
-            nc.vector.tensor_scalar(twice_pos[:], keep_f, 0.0, 2.0, ALU.is_ge, ALU.mult)
+            nc.vector.tensor_scalar(mant[:], keep_f[:].bitcast(I32), 0x7FFFFF, 0x3F800000, ALU.bitwise_and, ALU.bitwise_or)
+            nc.vector.tensor_scalar(expo[:], keep_f[:].bitcast(I32), 23, 0xFF, ALU.logical_shift_right, ALU.bitwise_and)
+            nc.vector.tensor_scalar(twice_pos[:], keep_f[:], 0.0, 2.0, ALU.is_ge, ALU.mult)
             nc.scalar.activation(ln_mant[:], mant[:].bitcast(F32), ACT.Ln)
+            warm = sb("warm", [P, SP, PACK], F32)
+            nc.scalar.activation(warm[:], ln_mant[:], ACT.Exp)
             nc.vector.tensor_scalar(ln_expo[:], expo[:], -127.0, math.log(2.0), ALU.add, ALU.mult)
-            nc.vector.scalar_tensor_tensor(signed_beta[:], twice_pos[:], -1.0, beta_f, ALU.add, ALU.mult)
+            nc.vector.scalar_tensor_tensor(signed_beta[:], twice_pos[:], -1.0, beta_f[:], ALU.add, ALU.mult)
             nc.vector.tensor_tensor(ln_keep[:], ln_mant[:], ln_expo[:], ALU.add)
 
         def mx_pair(name, width):
@@ -139,13 +122,13 @@ def tile_list_fast_weight_write_kernel(tc, xT, wgt, offs, wk, wv_words, wv_scale
         picked = [[sb(f"picked{a}{b}", [P, PACK, PASS], F32) for b in range(SP)] for a in range(KP)]
         xg = [[sb(f"xg{a}{b}", [P, PACK * PASS], BF16) for b in range(SP)] for a in range(KP)]
         xq = [[mx_pair(f"xq{a}{b}", PASS) for b in range(SP)] for a in range(KP)]
-        wkg = [[sb(f"wkg{a}{h}", [P, PACK * H], BF16) for h in range(2)] for a in range(KP)]
-        wkq = [[mx_pair(f"wkq{a}{h}", H) for h in range(2)] for a in range(KP)]
+        wkg = [sb(f"wkg{h}", [P, KP * PACK * H], BF16) for h in range(2)]
+        wkq = [mx_pair(f"wkq{h}", KP * H) for h in range(2)]
         key_rows = [[sb(f"key_rows{b}{h}", [P, PACK, H], BF16) for h in range(2)] for b in range(SP)]
-        keyg = [[sb(f"keyg{b}{h}", [P, PACK * H], BF16) for h in range(2)] for b in range(SP)]
+        keyg = [sb(f"keyg{b}", [P, PACK * R], BF16) for b in range(SP)]
         keyq = [mx_pair(f"keyq{b}", R) for b in range(SP)]
-        valg = [sb(f"valg{c}", [P, SP * PASS], BF16) for c in range(NT)]
-        valq = [mx_pair(f"valq{c}", SP * P) for c in range(NT)]
+        valg = [sb(f"valg{b}", [P, PACK * N], BF16) for b in range(SP)]
+        valq = [mx_pair(f"valq{b}", N) for b in range(SP)]
         val_rows = {}
         banks = {}
         copy_on = {"S": nc.scalar.copy, "V": nc.vector.tensor_copy}
@@ -161,14 +144,9 @@ def tile_list_fast_weight_write_kernel(tc, xT, wgt, offs, wk, wv_words, wv_scale
             )
 
         def group_x(engine, a, b, tiles, lanes):
-            dst = xg[a][b][:].rearrange("p (t m e i) -> p m t e i", t=PACK, e=4, i=PACK)
-            src = picked[a][b][:].rearrange("p i (m t e) -> p m t e i", t=PACK, e=4)
-            copy_on[engine](dst[:, :, tiles, :, lanes], src[:, :, tiles, :, lanes])
-
-        def group_x_all(engine, a, b, tiles):
-            dst = xg[a][b][:].rearrange("p (t m e i) -> p m t i e", t=PACK, e=4, i=PACK)
-            src = picked[a][b][:].rearrange("p i (m t e) -> p m t i e", t=PACK, e=4)
-            copy_on[engine](dst[:, :, tiles], src[:, :, tiles])
+            dst = xg[a][b][:].rearrange("p (t m i) -> p m i t", t=PACK, i=PACK)
+            src = picked[a][b][:].rearrange("p i (m t) -> p m i t", t=PACK)
+            copy_on[engine](dst[:, :, lanes, tiles], src[:, :, lanes, tiles])
 
         def mx(dst, left, lcols, right_codes, right_scales, start, stop):
             nc.tensor.matmul_mx(
@@ -191,14 +169,12 @@ def tile_list_fast_weight_write_kernel(tc, xT, wgt, offs, wk, wv_words, wv_scale
                 a, i, b = n
                 cols = slice(b * PASS // 16, (b + 1) * PASS // 16)
                 nc.vector.tensor_tensor(picked[a][b][:, i, :], planes[a][i][:].indirect(offsets[:, cols]), weights[b][:], ALU.mult)
+            elif kind == "r":
+                group_x(engine, 0, n[0], slice(0, 4), slice(0, 4))
             elif kind == "p":
                 group_x(engine, 1, n[0], slice(0, 4), slice(0, 2))
             elif kind == "f":
-                a, b, h = n
-                if a == 0 or not True:
-                    group_x_all(engine, a, b, slice(2 * h, 2 * h + 2))
-                else:
-                    group_x(engine, a, b, slice(2 * h, 2 * h + 2), slice(2, 4))
+                group_x(engine, 1, n[1], slice(2 * n[2], 2 * n[2] + 2), slice(0, 4))
             elif kind == "qx" and len(n) == 2:
                 quantise(xq[n[0]][n[1]], 0, PASS, xg[n[0]][n[1]][:])
             elif kind == "qx":
@@ -206,10 +182,12 @@ def tile_list_fast_weight_write_kernel(tc, xT, wgt, offs, wk, wv_words, wv_scale
                 quantise(xq[a][b], h * 256, 256, xg[a][b][:, h * 1024 : (h + 1) * 1024])
             elif kind == "w":
                 a, h = n
-                interleave(engine, wkg[a][h][:], wk_raw[a][h][:])
+                interleave(engine, wkg[h][:, a * 1024 : (a + 1) * 1024], wk_raw[a][h][:])
+            elif kind == "qw" and len(n) == 1:
+                quantise(wkq[n[0]], 0, KP * H, wkg[n[0]][:])
             elif kind == "qw":
                 a, h = n
-                quantise(wkq[a][h], 0, H, wkg[a][h][:])
+                quantise(wkq[h], a * H, H, wkg[h][:, a * 1024 : (a + 1) * 1024])
             elif kind == "z":
                 b, h, u = n
                 bank = new_bank()
@@ -218,7 +196,7 @@ def tile_list_fast_weight_write_kernel(tc, xT, wgt, offs, wk, wv_words, wv_scale
                     t = 2 * u + d
                     for a in range(KP):
                         mx(bank[:, d * H : (d + 1) * H], xq[a][b], slice(t * P, (t + 1) * P),
-                           wkq[a][h][0][:].bitcast(E4M3), wkq[a][h][1][:], a == 0, a == KP - 1)
+                           wkq[h][0][:, a * H : (a + 1) * H].bitcast(E4M3), wkq[h][1][:, a * H : (a + 1) * H], a == 0, a == KP - 1)
             elif kind == "e":
                 b, h, u = n
                 bank = banks["z", b, h, u]
@@ -227,10 +205,27 @@ def tile_list_fast_weight_write_kernel(tc, xT, wgt, offs, wk, wv_words, wv_scale
                     nc.scalar.activation(key_rows[b][h][:, t, :], bank[:, d * H : (d + 1) * H], ACT.Exp, bias=ln_keep[:, b, t : t + 1])
             elif kind == "k":
                 b, h = n
-                interleave(engine, keyg[b][h][:], key_rows[b][h][:])
+                interleave(engine, keyg[b][:, h * 1024 : (h + 1) * 1024], key_rows[b][h][:])
+            elif kind == "qk" and len(n) == 1:
+                quantise(keyq[n[0]], 0, R, keyg[n[0]][:])
             elif kind == "qk":
                 b, h = n
-                quantise(keyq[b], h * H, H, keyg[b][h][:])
+                quantise(keyq[b], h * H, H, keyg[b][:, h * 1024 : (h + 1) * 1024])
+            elif kind == "ya" or kind == "yb":
+                b, t = n
+                a = 0 if kind == "ya" else 1
+                if a == 0:
+                    banks["y", b, t] = new_bank()
+                mx(banks["y", b, t][:], xq[a][b], slice(t * P, (t + 1) * P),
+                   wv_codes[:, a, 0:1024].bitcast(E2M1), wv_plane[:, a, 0:512], a == 0, a == KP - 1)
+            elif kind == "ws":
+                b, t = n
+                if b not in val_rows:
+                    val_rows[b] = sb(f"wide_rows{b}", [P, PACK, 512], BF16)
+                nc.scalar.activation(val_rows[b][:, t, :], banks["y", b, t][:], ACT.Copy, scale=signed_beta[:, b, t : t + 1])
+            elif kind == "wi":
+                b, u = n
+                interleave(engine, valg[b][:, u * 1024 : (u + 1) * 1024], val_rows[b][:, :, u * 256 : (u + 1) * 256])
             elif kind == "vm":
                 b, c = n
                 bank = new_bank()
@@ -248,7 +243,7 @@ def tile_list_fast_weight_write_kernel(tc, xT, wgt, offs, wk, wv_words, wv_scale
                                          scale=signed_beta[:, b, t : t + 1])
             elif kind == "vd":
                 b, c = n
-                dst = valg[c][:, b * PASS : (b + 1) * PASS]
+                dst = valg[b][:, c * PASS : (c + 1) * PASS]
                 if (b, c) in val_rows:
                     interleave(engine, dst, val_rows[b, c][:])
                 else:
@@ -258,24 +253,25 @@ def tile_list_fast_weight_write_kernel(tc, xT, wgt, offs, wk, wv_words, wv_scale
                         signed_beta[:, b, :].unsqueeze(1).broadcast_to([P, P, PACK]),
                         ALU.mult,
                     )
-            elif kind == "qv" and len(n) == 1:
-                quantise(valq[n[0]], 0, SP * P, valg[n[0]][:])
+            elif kind == "qu":
+                b, u = n
+                quantise(valq[b], u * 256, 256, valg[b][:, u * 1024 : (u + 1) * 1024])
             elif kind == "qv":
                 b, c = n
-                quantise(valq[c], b * P, P, valg[c][:, b * PASS : (b + 1) * PASS])
+                quantise(valq[b], c * P, P, valg[b][:, c * PASS : (c + 1) * PASS])
             elif kind == "fm":
                 c = n[0]
                 cols = slice(0, R) if len(n) == 1 else slice(n[1] * H, (n[1] + 1) * H)
                 bank = new_bank()
                 banks["o", word] = bank
                 for b in range(SP):
-                    mx(bank[:, cols], valq[c], slice(b * P, (b + 1) * P),
+                    mx(bank[:, cols], valq[b], slice(c * P, (c + 1) * P),
                        keyq[b][0][:, cols].bitcast(E4M3), keyq[b][1][:, cols], b == 0, b == SP - 1)
             else:
                 c = n[0]
                 cols = slice(0, R) if len(n) == 1 else slice(n[1] * H, (n[1] + 1) * H)
                 nc.vector.scalar_tensor_tensor(
-                    state[c][:, cols], state[c][:, cols], factors[:, 0, 8 + c : 9 + c],
+                    state[c][:, cols], state[c][:, cols], lam_f[:, c : c + 1],
                     banks["o", "fm" + word[2:]][:, cols], ALU.mult, ALU.add,
                 )
                 nc.sync.dma_start(out[c * P : (c + 1) * P, cols], state[c][:, cols])

@@ -26,7 +26,7 @@ NT = N // P
 H = R // 2
 
 ORDER = """
-g000:V g001:V g010:V g011:V c:V g021:V g020:V g030:V g031:V r0:S g100:V g110:V r1:S g111:V g120:V qx01:V
+c:V g000:V g001:V g010:V g011:V g021:V g020:V g030:V g031:V r0:S g100:V g110:V r1:S g111:V g120:V qx01:V
 g130:V g131:V f100:S qx00:V f101:S g101:V w00:S qx10:V g121:V w10:S vm04:P w11:V w01:S vm02:P qw0:V vd04:V
 f110:S vm03:P vd02:V vm05:P qw1:V f111:S z000:P vd05:V z001:P qv04:V z011:P e000:S vd03:V z010:P qv05:V e001:S
 qx11:V vm00:P e011:S qu01:V vm01:P k00:V e010:S vm12:P vd00:V z111:P vd01:V k01:S vm11:P vd12:V z110:P vd11:V
@@ -72,8 +72,8 @@ def tile_list_fast_weight_write_kernel(tc, xT, wgt, offs, wk, wv_words, wv_scale
             for a in range(KP):
                 nc.sync.dma_start(wk_raw[a][h][:], wk_rows[a][:, :, h * H : (h + 1) * H])
 
-        nc.gpsimd.dma_start(keep_f[:], keep.rearrange("(b p t) -> p b t", b=SP, t=PACK))
-        nc.gpsimd.dma_start(beta_f[:], beta.rearrange("(b p t) -> p b t", b=SP, t=PACK))
+        nc.scalar.dma_start(keep_f[:], keep.rearrange("(b p t) -> p b t", b=SP, t=PACK))
+        nc.scalar.dma_start(beta_f[:], beta.rearrange("(b p t) -> p b t", b=SP, t=PACK))
         for q in range(4):
             nc.gpsimd.dma_start(
                 wv_plane[32 * q : 32 * q + 4].bitcast(I32),

@@ -26,14 +26,13 @@ NT = N // P
 H = R // 2
 
 ORDER = """
-c:V g000:V g001:V g010:V g011:V g021:V g020:V g030:V g031:V r0:S g100:V g110:V r1:S g111:V g120:V qx01:V
-g130:V g131:V f100:S qx00:V f101:S g101:V w00:S qx10:V g121:V w10:S vm04:P w11:V w01:S vm02:P qw0:V vd04:V
-f110:S vm03:P vd02:V vm05:P qw1:V f111:S z000:P vd05:V z001:P qv04:V z011:P e000:S vd03:V z010:P qv05:V e001:S
-qx11:V vm00:P e011:S qu01:V vm01:P k00:V e010:S vm12:P vd00:V z111:P vd01:V k01:S vm11:P vd12:V z110:P vd11:V
-e111:S vm10:P qu00:V vm14:P e110:S qk01:V vd10:V vm15:P qk00:V k11:S z101:P qu10:V vd15:V z100:P e101:S vm13:P
-vd14:V qk11:V e100:S vd13:V fm11:P fm01:P qu12:V k10:S st11:V fm51:P st01:V fm41:P qu11:V st51:V fm21:P qk10:V
-fm31:P st41:V fm30:P st21:V fm50:P st31:V fm20:P st30:V fm40:P st50:V fm00:P fm10:P st40:V st00:V st10:V
-st20:V
+c:V g000:V g001:V g010:V g011:V g020:V g021:V g030:V g031:V r0:S r1:S g100:V g101:V g110:V g111:V g120:V
+g121:V W0:S qx00:V g130:V qw0:V f100:S f101:V g131:V ya00:P ya01:P ya02:P ya03:P y00:P y01:P w10:S qx100:V
+qx101:V f110:S yb00:P yb01:P yb02:P yb03:P w11:V qx01:V qw1:V f111:V vm04:P vm05:P ws00:S ws01:S ws02:S ws03:S
+z00:P z01:P z02:P z03:P qx110:V vd04:V vd05:V qx111:V e00:S e01:S e02:S e03:S z10:P z11:P vm14:P z12:P vm15:P
+z13:P vm12:P vm13:P vm10:P vm11:P e10:S e11:S e12:S e13:S k10:S wi00:S vs11:S vd11:S wi01:V qu02:V K0:V qu01:V
+vd14:V qk0:V vd15:V vd12:V qu12:V k11:V vd13:V qk1:V qu11:V vd10:V qu00:V qu10:V fa4:P fa5:P fa2:P fa3:P fm4:P
+fm5:P st4:V st5:V fm2:P fm3:P st2:V st3:V fm0:P fm1:P st0:V st1:V
 """.split()
 
 
@@ -52,7 +51,7 @@ def tile_list_fast_weight_write_kernel(tc, xT, wgt, offs, wk, wv_words, wv_scale
         offsets = held.tile([P, S // 16], U16, name="offsets")
         planes = [[sb(f"plane{a}{i}", [P, T], F32) for i in range(PACK)] for a in range(KP)]
         weights = [sb(f"weights{b}", [P, PASS], F32) for b in range(SP)]
-        wk_raw = [[sb(f"wk_raw{a}{h}", [P, PACK, H], F32) for h in range(2)] for a in range(KP)]
+        wk_raw = [sb(f"wk_raw{a}", [P, PACK, R], F32) for a in range(KP)]
         wv_codes = sb("wv_codes", [P, KP, 2 * N], U8)
         wv_plane = sb("wv_plane", [P, KP, N], U8)
         keep_f = sb("keep_f", [P, SP, PACK], F32)
@@ -68,9 +67,8 @@ def tile_list_fast_weight_write_kernel(tc, xT, wgt, offs, wk, wv_words, wv_scale
         def load_plane(a, i):
             nc.sync.dma_start(planes[a][i][:], x_planes[a, i])
 
-        def load_wk(h):
-            for a in range(KP):
-                nc.sync.dma_start(wk_raw[a][h][:], wk_rows[a][:, :, h * H : (h + 1) * H])
+        def load_wk(a):
+            nc.sync.dma_start(wk_raw[a][:], wk_rows[a])
 
         nc.scalar.dma_start(keep_f[:], keep.rearrange("(b p t) -> p b t", b=SP, t=PACK))
         nc.scalar.dma_start(beta_f[:], beta.rearrange("(b p t) -> p b t", b=SP, t=PACK))
@@ -81,7 +79,7 @@ def tile_list_fast_weight_write_kernel(tc, xT, wgt, offs, wk, wv_words, wv_scale
             )
 
         nc.sync.dma_start(offsets[:], offs)
-        for item in "x00 wA wB x01 x02 x03 x10 x11 x12 x13 wv wk0 wk1".split():
+        for item in "x00 wA wB x01 x02 x03 x10 x11 x12 wk0 x13 wv wk1".split():
             if item[0] == "x":
                 load_plane(int(item[1]), int(item[2]))
             elif item == "wA":
@@ -124,7 +122,7 @@ def tile_list_fast_weight_write_kernel(tc, xT, wgt, offs, wk, wv_words, wv_scale
         xq = [[mx_pair(f"xq{a}{b}", PASS) for b in range(SP)] for a in range(KP)]
         wkg = [sb(f"wkg{h}", [P, KP * PACK * H], BF16) for h in range(2)]
         wkq = [mx_pair(f"wkq{h}", KP * H) for h in range(2)]
-        key_rows = [[sb(f"key_rows{b}{h}", [P, PACK, H], BF16) for h in range(2)] for b in range(SP)]
+        key_rows = [sb(f"key_rows{b}", [P, PACK, R], BF16) for b in range(SP)]
         keyg = [sb(f"keyg{b}", [P, PACK * R], BF16) for b in range(SP)]
         keyq = [mx_pair(f"keyq{b}", R) for b in range(SP)]
         valg = [sb(f"valg{b}", [P, PACK * N], BF16) for b in range(SP)]
@@ -182,30 +180,35 @@ def tile_list_fast_weight_write_kernel(tc, xT, wgt, offs, wk, wv_words, wv_scale
                 quantise(xq[a][b], h * 256, 256, xg[a][b][:, h * 1024 : (h + 1) * 1024])
             elif kind == "w":
                 a, h = n
-                interleave(engine, wkg[h][:, a * 1024 : (a + 1) * 1024], wk_raw[a][h][:])
+                interleave(engine, wkg[a][:, h * 1024 : (h + 1) * 1024], wk_raw[a][:, :, h * H : (h + 1) * H])
             elif kind == "qw" and len(n) == 1:
                 quantise(wkq[n[0]], 0, KP * H, wkg[n[0]][:])
             elif kind == "qw":
                 a, h = n
                 quantise(wkq[h], a * H, H, wkg[h][:, a * 1024 : (a + 1) * 1024])
-            elif kind == "z":
-                b, h, u = n
-                bank = new_bank()
-                banks["z", b, h, u] = bank
-                for d in range(2):
-                    t = 2 * u + d
-                    for a in range(KP):
-                        mx(bank[:, d * H : (d + 1) * H], xq[a][b], slice(t * P, (t + 1) * P),
-                           wkq[h][0][:, a * H : (a + 1) * H].bitcast(E4M3), wkq[h][1][:, a * H : (a + 1) * H], a == 0, a == KP - 1)
+            elif kind == "W":
+                interleave(engine, wkg[n[0]][:], wk_raw[n[0]][:])
+            elif kind == "K":
+                interleave(engine, keyg[n[0]][:], key_rows[n[0]][:])
+            elif kind == "F":
+                group_x(engine, 1, n[0], slice(0, 4), slice(0, 4))
+            elif kind == "qU":
+                b = n[0]
+                quantise(valq[b], n[1] * P, (n[2] - n[1]) * P, valg[b][:, n[1] * PASS : n[2] * PASS])
+            elif kind == "y" or kind == "z":
+                b, t = n
+                first = 1 if ("z", b, t) in banks else 0
+                if first == 0:
+                    banks["z", b, t] = new_bank()
+                for a in range(first, 1 if kind == "y" else KP):
+                    mx(banks["z", b, t][:], xq[a][b], slice(t * P, (t + 1) * P),
+                       wkq[a][0][:].bitcast(E4M3), wkq[a][1][:], a == 0, a == KP - 1)
             elif kind == "e":
-                b, h, u = n
-                bank = banks["z", b, h, u]
-                for d in range(2):
-                    t = 2 * u + d
-                    nc.scalar.activation(key_rows[b][h][:, t, :], bank[:, d * H : (d + 1) * H], ACT.Exp, bias=ln_keep[:, b, t : t + 1])
+                b, t = n
+                nc.scalar.activation(key_rows[b][:, t, :], banks["z", b, t][:], ACT.Exp, bias=ln_keep[:, b, t : t + 1])
             elif kind == "k":
                 b, h = n
-                interleave(engine, keyg[b][:, h * 1024 : (h + 1) * 1024], key_rows[b][h][:])
+                interleave(engine, keyg[b][:, h * 1024 : (h + 1) * 1024], key_rows[b][:, :, h * H : (h + 1) * H])
             elif kind == "qk" and len(n) == 1:
                 quantise(keyq[n[0]], 0, R, keyg[n[0]][:])
             elif kind == "qk":
@@ -259,12 +262,14 @@ def tile_list_fast_weight_write_kernel(tc, xT, wgt, offs, wk, wv_words, wv_scale
             elif kind == "qv":
                 b, c = n
                 quantise(valq[b], c * P, P, valg[b][:, c * PASS : (c + 1) * PASS])
-            elif kind == "fm":
+            elif kind == "fm" or kind == "fa":
                 c = n[0]
                 cols = slice(0, R) if len(n) == 1 else slice(n[1] * H, (n[1] + 1) * H)
-                bank = new_bank()
-                banks["o", word] = bank
-                for b in range(SP):
+                first = 1 if ("o", "fm" + word[2:]) in banks else 0
+                if first == 0:
+                    banks["o", "fm" + word[2:]] = new_bank()
+                bank = banks["o", "fm" + word[2:]]
+                for b in range(first, 1 if kind == "fa" else SP):
                     mx(bank[:, cols], valq[b], slice(c * P, (c + 1) * P),
                        keyq[b][0][:, cols].bitcast(E4M3), keyq[b][1][:, cols], b == 0, b == SP - 1)
             else:

import math
from contextlib import ExitStack

import concourse.mybir as mybir

K, T, S, R, N = 1024, 2048, 1024, 512, 768
FLOPS = 2 * K * S * R + 2 * K * S * N + 2 * S * N * R

F32 = mybir.dt.float32
BF16 = mybir.dt.bfloat16
I32 = mybir.dt.int32
U32 = mybir.dt.uint32
U16 = mybir.dt.uint16
U8 = mybir.dt.uint8
E4M3 = mybir.dt.float8_e4m3fn_x4
E2M1 = mybir.dt.float4_e2m1fn_x4
ALU = mybir.AluOpType
ACT = mybir.ActivationFunctionType

P = 128
PACK = 4
PASS = P * PACK
KP = K // PASS
SP = S // PASS
NT = N // P
H = R // 2

ORDER = """
c:V g000:V g001:V g010:V g011:V g020:V g021:V g030:V g031:V r0:S r1:S g100:V g101:V g110:V g111:V g120:V
g121:V W0:S qx00:V g130:V qw0:V f100:S f101:V g131:V ya00:P ya01:P ya02:P ya03:P y00:P y01:P w10:S qx100:V
qx101:V f110:S yb00:P yb01:P yb02:P yb03:P w11:V qx01:V qw1:V f111:V vm04:P vm05:P ws00:S ws01:S ws02:S ws03:S
z00:P z01:P z02:P z03:P qx110:V vd04:V vd05:V qx111:V e00:S e01:S e02:S e03:S z10:P z11:P vm14:P z12:P vm15:P
z13:P vm12:P vm13:P vm10:P vm11:P e10:S e11:S e12:S e13:S k10:S wi00:S vs11:S vd11:S wi01:V qu02:V K0:V qu01:V
vd14:V qk0:V vd15:V vd12:V qu12:V k11:V vd13:V qk1:V qu11:V vd10:V qu00:V qu10:V fa4:P fa5:P fa2:P fa3:P fm4:P
fm5:P st4:V st5:V fm2:P fm3:P st2:V st3:V fm0:P fm1:P st0:V st1:V
""".split()


def tile_list_fast_weight_write_kernel(tc, xT, wgt, offs, wk, wv_words, wv_scales, keep, beta, lam, old, out):
    nc = tc.nc
    with ExitStack() as ctx:
        held = ctx.enter_context(tc.tile_pool(name="held", bufs=1))
        psum = ctx.enter_context(tc.psum_pool(name="psum", bufs=8))

        def sb(name, shape, dtype):
            return held.tile(shape, dtype, name=name, align_bytes=64)

        def new_bank():
            return psum.tile([P, 512], F32, name="bank")

        offsets = held.tile([P, S // 16], U16, name="offsets")
        planes = [[sb(f"plane{a}{i}", [P, T], F32) for i in range(PACK)] for a in range(KP)]
        weights = [sb(f"weights{b}", [P, PASS], F32) for b in range(SP)]
        wk_raw = [sb(f"wk_raw{a}", [P, PACK, R], F32) for a in range(KP)]
        wv_codes = sb("wv_codes", [P, KP, 2 * N], U8)
        wv_plane = sb("wv_plane", [P, KP, N], U8)
        keep_f = sb("keep_f", [P, SP, PACK], F32)
        beta_f = sb("beta_f", [P, SP, PACK], F32)
        lam_f = sb("lam_f", [P, NT], F32)
        state = [sb(f"state{c}", [P, R], F32) for c in range(NT)]

        nc.gpsimd.memset(wv_plane[:].rearrange("p a n -> p (a n)").bitcast(I32), 0)

        x_planes = xT.rearrange("(a p i) t -> a i p t", a=KP, i=PACK)
        wk_rows = wk.rearrange("(a p i) r -> a p i r", a=KP, i=PACK)

        def load_plane(a, i):
            nc.sync.dma_start(planes[a][i][:], x_planes[a, i])

        def load_wk(a):
            nc.sync.dma_start(wk_raw[a][:], wk_rows[a])

        nc.scalar.dma_start(keep_f[:], keep.rearrange("(b p t) -> p b t", b=SP, t=PACK))
        nc.scalar.dma_start(beta_f[:], beta.rearrange("(b p t) -> p b t", b=SP, t=PACK))
        for q in range(4):
            nc.gpsimd.dma_start(
                wv_plane[32 * q : 32 * q + 4].bitcast(I32),
                wv_scales[:, 4 * q : 4 * q + 4, :].rearrange("a r n -> r a n").bitcast(I32),
            )

        nc.sync.dma_start(offsets[:], offs)
        for item in "x00 wA wB x01 x02 x03 x10 x11 x12 wk0 x13 wv wk1".split():
            if item[0] == "x":
                load_plane(int(item[1]), int(item[2]))
            elif item == "wA":
                nc.sync.dma_start(weights[0][:], wgt[:, 0:PASS])
            elif item == "wB":
                nc.sync.dma_start(weights[1][:], wgt[:, PASS:S])
            elif item == "wv":
                nc.sync.dma_start(wv_codes[:].bitcast(I32), wv_words.rearrange("a p n -> p a n").bitcast(I32))
            else:
                load_wk(int(item[2]))
        with nc.allow_non_contiguous_dma(reason="one decay factor to a partition"):
            nc.sync.dma_start(lam_f[:], lam.rearrange("(c p) -> p c", p=P))
        for c in range(NT):
            nc.sync.dma_start(state[c][:], old[c * P : (c + 1) * P, :])

        ln_keep = sb("ln_keep", [P, SP, PACK], F32)
        signed_beta = sb("signed_beta", [P, SP, PACK], F32)

        def make_factors():
            expo = sb("expo", [P, SP, PACK], I32)
            mant = sb("mant", [P, SP, PACK], I32)
            ln_expo = sb("ln_expo", [P, SP, PACK], F32)
            ln_mant = sb("ln_mant", [P, SP, PACK], F32)
            twice_pos = sb("twice_pos", [P, SP, PACK], F32)
            nc.vector.tensor_scalar(mant[:], keep_f[:].bitcast(I32), 0x7FFFFF, 0x3F800000, ALU.bitwise_and, ALU.bitwise_or)
            nc.vector.tensor_scalar(expo[:], keep_f[:].bitcast(I32), 23, 0xFF, ALU.logical_shift_right, ALU.bitwise_and)
            nc.vector.tensor_scalar(twice_pos[:], keep_f[:], 0.0, 2.0, ALU.is_ge, ALU.mult)
            nc.scalar.activation(ln_mant[:], mant[:].bitcast(F32), ACT.Ln)
            warm = sb("warm", [P, SP, PACK], F32)
            nc.scalar.activation(warm[:], ln_mant[:], ACT.Exp)
            nc.vector.tensor_scalar(ln_expo[:], expo[:], -127.0, math.log(2.0), ALU.add, ALU.mult)
            nc.vector.scalar_tensor_tensor(signed_beta[:], twice_pos[:], -1.0, beta_f[:], ALU.add, ALU.mult)
            nc.vector.tensor_tensor(ln_keep[:], ln_mant[:], ln_expo[:], ALU.add)

        def mx_pair(name, width):
            return sb(name + "_codes", [P, width], U32), sb(name + "_scales", [P, width], U8)

        picked = [[sb(f"picked{a}{b}", [P, PACK, PASS], F32) for b in range(SP)] for a in range(KP)]
        xg = [[sb(f"xg{a}{b}", [P, PACK * PASS], BF16) for b in range(SP)] for a in range(KP)]
        xq = [[mx_pair(f"xq{a}{b}", PASS) for b in range(SP)] for a in range(KP)]
        wkg = [sb(f"wkg{h}", [P, KP * PACK * H], BF16) for h in range(2)]
        wkq = [mx_pair(f"wkq{h}", KP * H) for h in range(2)]
        key_rows = [sb(f"key_rows{b}", [P, PACK, R], BF16) for b in range(SP)]
        keyg = [sb(f"keyg{b}", [P, PACK * R], BF16) for b in range(SP)]
        keyq = [mx_pair(f"keyq{b}", R) for b in range(SP)]
        valg = [sb(f"valg{b}", [P, PACK * N], BF16) for b in range(SP)]
        valq = [mx_pair(f"valq{b}", N) for b in range(SP)]
        val_rows = {}
        banks = {}
        copy_on = {"S": nc.scalar.copy, "V": nc.vector.tensor_copy}

        def quantise(pair, first, width, grouped):
            cols = slice(first, first + width)
            nc.vector.quantize_mx(pair[0][:, cols].bitcast(E4M3), pair[1][:, cols], grouped)

        def interleave(engine, dst, src):
            copy_on[engine](
                dst.rearrange("p (c e t) -> p c t e", t=PACK, e=4),
                src.rearrange("p t (c e) -> p c t e", e=4),
            )

        def group_x(engine, a, b, tiles, lanes):
            dst = xg[a][b][:].rearrange("p (t m i) -> p m i t", t=PACK, i=PACK)
            src = picked[a][b][:].rearrange("p i (m t) -> p m i t", t=PACK)
            copy_on[engine](dst[:, :, lanes, tiles], src[:, :, lanes, tiles])

        def mx(dst, left, lcols, right_codes, right_scales, start, stop):
            nc.tensor.matmul_mx(
                dst,
                lhsT=left[0][:, lcols].bitcast(E4M3),
                lhsT_scale=left[1][:, lcols],
                rhs=right_codes,
                rhs_scale=right_scales,
                start=start,
                stop=stop,
            )

        for step in ORDER:
            word, engine = step.split(":")
            kind = "".join(ch for ch in word if ch not in "0123456789")
            n = [int(ch) for ch in word if ch in "0123456789"]
            if kind == "c":
                make_factors()
            elif kind == "g":
                a, i, b = n
                cols = slice(b * PASS // 16, (b + 1) * PASS // 16)
                nc.vector.tensor_tensor(picked[a][b][:, i, :], planes[a][i][:].indirect(offsets[:, cols]), weights[b][:], ALU.mult)
            elif kind == "r":
                group_x(engine, 0, n[0], slice(0, 4), slice(0, 4))
            elif kind == "p":
                group_x(engine, 1, n[0], slice(0, 4), slice(0, 2))
            elif kind == "f":
                group_x(engine, 1, n[1], slice(2 * n[2], 2 * n[2] + 2), slice(0, 4))
            elif kind == "qx" and len(n) == 2:
                quantise(xq[n[0]][n[1]], 0, PASS, xg[n[0]][n[1]][:])
            elif kind == "qx":
                a, b, h = n
                quantise(xq[a][b], h * 256, 256, xg[a][b][:, h * 1024 : (h + 1) * 1024])
            elif kind == "w":
                a, h = n
                interleave(engine, wkg[a][:, h * 1024 : (h + 1) * 1024], wk_raw[a][:, :, h * H : (h + 1) * H])
            elif kind == "qw" and len(n) == 1:
                quantise(wkq[n[0]], 0, KP * H, wkg[n[0]][:])
            elif kind == "qw":
                a, h = n
                quantise(wkq[h], a * H, H, wkg[h][:, a * 1024 : (a + 1) * 1024])
            elif kind == "W":
                interleave(engine, wkg[n[0]][:], wk_raw[n[0]][:])
            elif kind == "K":
                interleave(engine, keyg[n[0]][:], key_rows[n[0]][:])
            elif kind == "F":
                group_x(engine, 1, n[0], slice(0, 4), slice(0, 4))
            elif kind == "qU":
                b = n[0]
                quantise(valq[b], n[1] * P, (n[2] - n[1]) * P, valg[b][:, n[1] * PASS : n[2] * PASS])
            elif kind == "y" or kind == "z":
                b, t = n
                first = 1 if ("z", b, t) in banks else 0
                if first == 0:
                    banks["z", b, t] = new_bank()
                for a in range(first, 1 if kind == "y" else KP):
                    mx(banks["z", b, t][:], xq[a][b], slice(t * P, (t + 1) * P),
                       wkq[a][0][:].bitcast(E4M3), wkq[a][1][:], a == 0, a == KP - 1)
            elif kind == "e":
                b, t = n
                nc.scalar.activation(key_rows[b][:, t, :], banks["z", b, t][:], ACT.Exp, bias=ln_keep[:, b, t : t + 1])
            elif kind == "k":
                b, h = n
                interleave(engine, keyg[b][:, h * 1024 : (h + 1) * 1024], key_rows[b][:, :, h * H : (h + 1) * H])
            elif kind == "qk" and len(n) == 1:
                quantise(keyq[n[0]], 0, R, keyg[n[0]][:])
            elif kind == "qk":
                b, h = n
                quantise(keyq[b], h * H, H, keyg[b][:, h * 1024 : (h + 1) * 1024])
            elif kind == "ya" or kind == "yb":
                b, t = n
                a = 0 if kind == "ya" else 1
                if a == 0:
                    banks["y", b, t] = new_bank()
                mx(banks["y", b, t][:], xq[a][b], slice(t * P, (t + 1) * P),
                   wv_codes[:, a, 0:1024].bitcast(E2M1), wv_plane[:, a, 0:512], a == 0, a == KP - 1)
            elif kind == "ws":
                b, t = n
                if b not in val_rows:
                    val_rows[b] = sb(f"wide_rows{b}", [P, PACK, 512], BF16)
                nc.scalar.activation(val_rows[b][:, t, :], banks["y", b, t][:], ACT.Copy, scale=signed_beta[:, b, t : t + 1])
            elif kind == "wi":
                b, u = n
                interleave(engine, valg[b][:, u * 1024 : (u + 1) * 1024], val_rows[b][:, :, u * 256 : (u + 1) * 256])
            elif kind == "vm":
                b, c = n
                bank = new_bank()
                banks["v", b, c] = bank
                for t in range(PACK):
                    for a in range(KP):
                        mx(bank[:, t * P : (t + 1) * P], xq[a][b], slice(t * P, (t + 1) * P),
                           wv_codes[:, a, 2 * c * P : 2 * (c + 1) * P].bitcast(E2M1), wv_plane[:, a, c * P : (c + 1) * P],
                           a == 0, a == KP - 1)
            elif kind == "vs":
                b, c = n
                val_rows[b, c] = sb(f"val_rows{b}{c}", [P, PACK, P], BF16)
                for t in range(PACK):
                    nc.scalar.activation(val_rows[b, c][:, t, :], banks["v", b, c][:, t * P : (t + 1) * P], ACT.Copy,
                                         scale=signed_beta[:, b, t : t + 1])
            elif kind == "vd":
                b, c = n
                dst = valg[b][:, c * PASS : (c + 1) * PASS]
                if (b, c) in val_rows:
                    interleave(engine, dst, val_rows[b, c][:])
                else:
                    nc.vector.tensor_tensor(
                        dst.rearrange("p (n t) -> p n t", t=PACK),
                        banks["v", b, c][:].rearrange("p (t n) -> p n t", t=PACK),
                        signed_beta[:, b, :].unsqueeze(1).broadcast_to([P, P, PACK]),
                        ALU.mult,
                    )
            elif kind == "qu":
                b, u = n
                quantise(valq[b], u * 256, 256, valg[b][:, u * 1024 : (u + 1) * 1024])
            elif kind == "qv":
                b, c = n
                quantise(valq[b], c * P, P, valg[b][:, c * PASS : (c + 1) * PASS])
            elif kind == "fm" or kind == "fa":
                c = n[0]
                cols = slice(0, R) if len(n) == 1 else slice(n[1] * H, (n[1] + 1) * H)
                first = 1 if ("o", "fm" + word[2:]) in banks else 0
                if first == 0:
                    banks["o", "fm" + word[2:]] = new_bank()
                bank = banks["o", "fm" + word[2:]]
                for b in range(first, 1 if kind == "fa" else SP):
                    mx(bank[:, cols], valq[b], slice(c * P, (c + 1) * P),
                       keyq[b][0][:, cols].bitcast(E4M3), keyq[b][1][:, cols], b == 0, b == SP - 1)
            else:
                c = n[0]
                cols = slice(0, R) if len(n) == 1 else slice(n[1] * H, (n[1] + 1) * H)
                nc.vector.scalar_tensor_tensor(
                    state[c][:, cols], state[c][:, cols], lam_f[:, c : c + 1],
                    banks["o", "fm" + word[2:]][:, cols], ALU.mult, ALU.add,
                )
                nc.sync.dma_start(out[c * P : (c + 1) * P, cols], state[c][:, cols])
